import numpy as np
import ml_dtypes


def mxq(x, axis, fmt="e4m3"):
    dtype, down = {"e4m3": (ml_dtypes.float8_e4m3fn, 7), "e5m2": (ml_dtypes.float8_e5m2, 14)}[fmt]
    v = np.moveaxis(np.asarray(x, np.float32).astype(ml_dtypes.bfloat16).astype(np.float64), axis, -1)
    blocks = v.reshape(v.shape[:-1] + (-1, 32))
    amax = np.abs(blocks).max(-1, keepdims=True)
    byte = np.maximum(np.where(amax > 0, np.frexp(amax)[1] - 1 + 127, 0) - down, 1)
    scale = np.exp2(byte - 127.0)
    codes = (blocks / scale).astype(np.float32).astype(dtype).astype(np.float64)
    return np.moveaxis((codes * scale).reshape(v.shape), -1, axis)


WIDE = False


def mx_kscale(k):
    if not WIDE:
        return np.ones(k)
    levels = np.array([10, -10, 5, -5, 0])
    if k % 512:
        return np.exp2(np.random.permutation(np.resize(levels, k // 32))).repeat(32)
    a = np.empty((k // 512, 16))
    for p in range(k // 512):
        a[p, :8] = np.random.permutation(np.resize(levels, 8))
        for g in range(8):
            far = levels[np.abs(levels - a[p, g]) >= 10]
            a[p, g + 8] = far[np.random.randint(len(far))]
    return np.exp2(a.ravel()).repeat(32)


def f64(x):
    return np.asarray(x).astype(np.float64)


def striped(idx):
    return np.tile(idx.reshape(-1, 16).T, (8, 1)).astype(np.uint16)


def unstriped(offs):
    return offs[:16].T.reshape(-1).astype(np.int64)


def striped8(idx):
    return np.concatenate([x.reshape(-1, 16).T for x in idx]).astype(np.uint16)


def runs(offs, k):
    lists = np.stack([offs[16 * r : 16 * r + 16].T.reshape(-1) for r in range(8)]).astype(np.int64)
    return lists[np.arange(k) % 512 // 64]


def pack_weight(w):
    k, n = w.shape
    w = f64(np.asarray(w, np.float32).astype(ml_dtypes.bfloat16)).reshape(k // 32, 32, n)
    amax = np.abs(w).max(1)
    byte = np.clip(np.where(amax > 0, np.frexp(amax)[1] - 1 + 127 - 7, 1), 1, 254)
    scaled = (w * np.exp2(127.0 - byte)[:, None, :]).reshape(k, n).astype(np.float32)
    words = np.ascontiguousarray(scaled.reshape(k // 512, 128, 4, n).transpose(0, 1, 3, 2)).astype(ml_dtypes.float8_e4m3fn).view(np.uint8)
    return words, np.ascontiguousarray(byte.astype(np.uint8).reshape(k // 512, 16, n))


def unpack_weight(words, scales):
    g, p, n, _ = words.shape
    vals = np.ascontiguousarray(words).view(ml_dtypes.float8_e4m3fn).astype(np.float64) * np.repeat(np.exp2(scales.astype(np.float64) - 127.0), 8, axis=1)[..., None]
    return vals.transpose(0, 1, 3, 2).reshape(g * 512, n)


E2M1 = np.array([0.0, 0.5, 1.0, 1.5, 2.0, 3.0, 4.0, 6.0, -0.0, -0.5, -1.0, -1.5, -2.0, -3.0, -4.0, -6.0])


def pack_fp4(w):
    k, n = w.shape
    w = f64(np.asarray(w, np.float32).astype(ml_dtypes.bfloat16)).reshape(k // 32, 32, n)
    amax = np.abs(w).max(1)
    mant, ex = np.frexp(amax / 6.0)
    byte = np.clip(np.where(amax > 0, np.where(mant > 0.5, ex, ex - 1) + 127, 1), 1, 254)
    scaled = (w * np.exp2(127.0 - byte)[:, None, :]).reshape(k, n).astype(np.float32)
    c = np.ascontiguousarray(scaled.reshape(k // 512, 128, 4, n).transpose(0, 1, 3, 2)).astype(ml_dtypes.float4_e2m1fn).view(np.uint8) & 0xF
    words = (c[..., 0::2] | (c[..., 1::2] << 4)).reshape(k // 512, 128, 2 * n)
    return np.ascontiguousarray(words), np.ascontiguousarray(byte.astype(np.uint8).reshape(k // 512, 16, n))


def unpack_fp4(words, scales):
    g, _, n = scales.shape
    words = np.ascontiguousarray(words).reshape(g, 128, n, 2)
    nib = np.empty((g, 128, n, 4), np.uint8)
    nib[..., 0::2] = words & 0xF
    nib[..., 1::2] = words >> 4
    vals = E2M1[nib] * np.repeat(np.exp2(scales.astype(np.float64) - 127.0), 8, axis=1)[..., None]
    return vals.transpose(0, 1, 3, 2).reshape(g * 512, n)


def planes(y):
    n, m = y.shape
    v = y.astype(np.float32).astype(ml_dtypes.bfloat16).astype(np.float64).reshape(n // 32, 32, m)
    top = np.abs(v).max(1)
    byte = np.clip(np.where(top > 0, np.frexp(top)[1] - 1 + 127 - 7, 1), 1, 254)
    codes = (v * np.exp2(127.0 - byte)[:, None, :]).reshape(n, m).astype(np.float32).astype(ml_dtypes.float8_e4m3fn).view(np.uint8)
    words = codes.reshape(n // 512, 128, 4, m).transpose(0, 1, 3, 2)
    return np.ascontiguousarray(words), np.ascontiguousarray(byte.astype(np.uint8).reshape(n // 512, 16, m))


K, T, S, H, J, C = 512, 2048, 512, 512, 512, 512


def setup_inputs():
    n = np.random.standard_normal
    s = mx_kscale(K)[:, None]
    packed_xT = pack_weight(n((K, T)) * s)
    packed_w1 = pack_fp4(n((K, H)) / np.sqrt(K) / s)
    return {
        "x_words": packed_xT[0],
        "x_scales": packed_xT[1],
        "w1_words": packed_w1[0],
        "w1_scales": packed_w1[1],
        "tab": n((H, J)).astype(np.float32),
        "gs": (np.random.uniform(0.5, 1.5, (K, 1)) / s).astype(np.float32),
        "offs": striped(np.random.permutation(T)[:S]),
        "n1": striped8(np.random.randint(0, J, (8, S))),
        "n2": striped8(np.random.randint(0, J, (8, S))),
        "n3": striped8(np.stack([np.random.permutation(S) for _ in range(8)])),
        "cand": striped(np.random.permutation(T)[:C]),
        "n4": striped8(np.stack([np.random.permutation(S) for _ in range(8)])),
        "n5": striped8(np.stack([np.random.permutation(S) for _ in range(8)])),
        "n6": striped8(np.stack([np.random.permutation(S) for _ in range(8)])),
    }


def reference(x_words, x_scales, w1_words, w1_scales, tab, gs, offs, n1, n2, n3, cand, n4, n5, n6):
    x_cand = unpack_weight(x_words, x_scales)[:, unstriped(cand)]
    xq = unpack_weight(x_words, x_scales)[:, unstriped(offs)]
    y = unpack_fp4(w1_words, w1_scales).T @ xq
    z = f64(gs) * ((y[np.arange(H)[:, None], runs(n3, H)]) * (f64(tab)[np.arange(H)[:, None], runs(n1, H)]) + f64(tab)[np.arange(H)[:, None], runs(n2, H)])
    s = 0.0625 * ((x_cand.T @ mxq(z, 0, "e4m3")))
    out_0 = s + s[np.arange(C)[:, None], runs(n4, C)] - (np.maximum(s[np.arange(C)[:, None], runs(n5, C)], s[np.arange(C)[:, None], runs(n6, C)]))
    return (out_0,) + planes(out_0)

@@ -1,0 +1,299 @@
+from contextlib import ExitStack
+
+import concourse.mybir as mybir
+
+K, T, S, H, J, C = 512, 2048, 512, 512, 512, 512
+FLOPS = 2 * K * H * S + 2 * K * C * S
+
+F32 = mybir.dt.float32
+BF16 = mybir.dt.bfloat16
+I32 = mybir.dt.int32
+U32 = mybir.dt.uint32
+U16 = mybir.dt.uint16
+U8 = mybir.dt.uint8
+FP8X4 = mybir.dt.float8_e4m3fn_x4
+FP4X4 = mybir.dt.float4_e2m1fn_x4
+ALU = mybir.AluOpType
+COPY = mybir.ActivationFunctionType.Copy
+
+P = 128
+PACK = 4
+QUADS = 4
+CHUNKS = ((0, 256), (256, 128), (384, 128))
+LAST = len(CHUNKS) - 1
+HALF = 256
+
+
+def entries(offsets, start, width):
+    return offsets[:, start // 16 : (start + width) // 16]
+
+
+def tile_picked_candkindatrim_none_po_kernel(
+    tc, x_words, x_scales, w1_words, w1_scales, tab, gs, offs, n1, n2, n3, cand, n4, n5, n6, out_0, out_1, out_2
+):
+    nc = tc.nc
+    with ExitStack() as ctx:
+        keep = ctx.enter_context(tc.tile_pool(name="keep", bufs=1))
+        psum = ctx.enter_context(tc.psum_pool(name="psum", bufs=1))
+
+        def sb(shape, dtype, name, tag=None):
+            return keep.tile(shape, dtype, name=name, tag=tag or name, align_bytes=64)
+
+        def load_list(src, name):
+            offsets = keep.tile([P, S // 16], U16, name=name)
+            nc.sync.dma_start(offsets[:], src)
+            return offsets
+
+        def load_scales(dst, src):
+            for q in range(QUADS):
+                nc.sync.dma_start(dst[32 * q : 32 * q + 4, :].bitcast(I32), src[0, 4 * q : 4 * q + 4, :].bitcast(I32))
+
+        def interleave(engine_copy, dst, src):
+            engine_copy(
+                dst[:].rearrange("p (c i t) -> p c t i", i=4, t=PACK),
+                src[:].rearrange("p t (c i) -> p c t i", i=4),
+            )
+
+        xs = sb([P, T], U8, "xs")
+        nc.vector.memset(xs[:].bitcast(I32), 0)
+        w1s = sb([P, H], U8, "w1s")
+        nc.gpsimd.memset(w1s[:].bitcast(I32), 0)
+
+        w1w = sb([P, 2 * H], U8, "w1w")
+        nc.sync.dma_start(w1w[:].bitcast(I32), w1_words[0].bitcast(I32))
+        n1_t = load_list(n1, "n1_t")
+        tab_rows = tab.rearrange("(p t) j -> p t j", t=PACK)
+        tabs = []
+        for t in range(PACK):
+            tile = sb([P, J], F32, "tab%d" % t)
+            nc.sync.dma_start(tile[:], tab_rows[:, t, :])
+            tabs.append(tile)
+        xw = sb([P, T], I32, "xw")
+        nc.sync.dma_start(xw[:], x_words[0].rearrange("p n t -> p (n t)").bitcast(I32))
+        offs_t = load_list(offs, "offs_t")
+        load_scales(xs, x_scales)
+        load_scales(w1s, w1_scales)
+        gs_t = sb([P, PACK], F32, "gs_t")
+        nc.sync.dma_start(gs_t[:], gs.rearrange("(p t) o -> p (t o)", t=PACK))
+        cand_t = load_list(cand, "cand_t")
+        n3_t = load_list(n3, "n3_t")
+        n2_t = load_list(n2, "n2_t")
+        n6_t = load_list(n6, "n6_t")
+        n5_t = load_list(n5, "n5_t")
+        n4_t = load_list(n4, "n4_t")
+
+        w1w_d = sb([P, 2 * H], U8, "w1w_d")
+        nc.vector.tensor_copy(
+            w1w_d[:].rearrange("p (t m b) -> p t m b", t=PACK, b=2),
+            w1w[:].rearrange("p (m t b) -> p t m b", t=PACK, b=2),
+        )
+
+        kind1 = []
+        for t in range(PACK):
+            tile = sb([P, S], F32, "kind1_%d" % t)
+            for h in range(0, S, HALF):
+                nc.vector.tensor_copy(tile[:, h : h + HALF], tabs[t][:].indirect(entries(n1_t, h, HALF)))
+            kind1.append(tile)
+
+        tabg = []
+        for t in range(PACK):
+            tile = sb([P, J], F32, "tabg%d" % t)
+            nc.scalar.activation(tile[:], tabs[t][:], COPY, scale=gs_t[:, t : t + 1])
+            tabg.append(tile)
+
+        xq_w = sb([P, S], I32, "xq_w")
+        nc.vector.tensor_copy(xq_w[:].bitcast(U32), xw[:].bitcast(U32).indirect(offs_t[:]))
+        xq_s = sb([P, S], U8, "xq_s")
+        nc.vector.tensor_copy(xq_s[:], xs[:].indirect(offs_t[:]))
+        w1s_d = sb([P, H], U8, "w1s_d")
+        nc.vector.tensor_copy(
+            w1s_d[:].rearrange("p (t m) -> p t m", t=PACK), w1s[:].rearrange("p (m t) -> p t m", t=PACK)
+        )
+
+        ys = []
+        for t in range(PACK):
+            bank = psum.tile([P, S], F32, name="y_ps%d" % t, tag="bank%d" % t)
+            nc.tensor.matmul_mx(
+                bank[:],
+                lhsT=w1w_d[:, 2 * P * t : 2 * P * (t + 1)].bitcast(FP4X4),
+                lhsT_scale=w1s_d[:, P * t : P * (t + 1)],
+                rhs=xq_w[:].bitcast(FP8X4),
+                rhs_scale=xq_s[:],
+                start=True,
+                stop=True,
+            )
+            tile = sb([P, S], F32, "y%d" % t)
+            nc.scalar.activation(tile[:], bank[:], COPY, scale=gs_t[:, t : t + 1])
+            ys.append(tile)
+
+        xc_w = sb([P, C], I32, "xc_w")
+        nc.vector.tensor_copy(xc_w[:].bitcast(U32), xw[:].bitcast(U32).indirect(cand_t[:]))
+        xc_s = sb([P, C], U8, "xc_s")
+        nc.vector.tensor_copy(xc_s[:], xs[:].indirect(cand_t[:]))
+        xc_wd = sb([P, C], I32, "xc_wd")
+        nc.vector.tensor_copy(
+            xc_wd[:].rearrange("p (t m) -> p t m", t=PACK), xc_w[:].rearrange("p (m t) -> p t m", t=PACK)
+        )
+        xc_sd = sb([P, C], U8, "xc_sd")
+        nc.vector.tensor_copy(
+            xc_sd[:].rearrange("p (t m) -> p t m", t=PACK), xc_s[:].rearrange("p (m t) -> p t m", t=PACK)
+        )
+
+        z_f32 = [sb([P, PACK, w], F32, "z%d" % c) for c, (start, w) in enumerate(CHUNKS)]
+        s_win = [sb([P, S], F32, "s_win%d" % t) for t in range(PACK)]
+        s_own = [sb([P, PACK, w], F32, "s_own%d" % c) for c, (start, w) in enumerate(CHUNKS)]
+        prods = {}
+        z_bf = {}
+        s_ps = {}
+
+        def prod(c, t, tag=None):
+            start, w = CHUNKS[c]
+            tile = sb([P, w], F32, "prod%d_%d" % (c, t), tag)
+            nc.vector.tensor_tensor(
+                tile[:], ys[t][:].indirect(entries(n3_t, start, w)), kind1[t][:, start : start + w], ALU.mult
+            )
+            prods[c, t] = tile
+
+        def zsum(c, t):
+            start, w = CHUNKS[c]
+            nc.vector.tensor_tensor(
+                z_f32[c][:, t, :], tabg[t][:].indirect(entries(n2_t, start, w)), prods[c, t][:], ALU.add
+            )
+
+        def z_round(c):
+            w = CHUNKS[c][1]
+            z_bf[c] = sb([P, PACK * w], BF16, "z_bf%d" % c)
+            interleave(nc.vector.tensor_copy if c == LAST else nc.scalar.copy, z_bf[c], z_f32[c])
+
+        def z_product(c):
+            w = CHUNKS[c][1]
+            codes = sb([P, w], U32, "z_codes%d" % c)
+            scales = sb([P, w], U8, "z_scales%d" % c)
+            nc.vector.quantize_mx(codes[:].bitcast(FP8X4), scales[:], z_bf[c][:])
+            per_bank = 1 if c == LAST else 512 // w
+            first_bank = (4, 6, 0)[c]
+            for b in range(PACK // per_bank):
+                bank = psum.tile([P, per_bank, w], F32, name="s_ps%d_%d" % (c, b), tag="bank%d" % (first_bank + b))
+                s_ps[c, b] = bank
+                for i in range(per_bank):
+                    t = b * per_bank + i
+                    nc.tensor.matmul_mx(
+                        bank[:, i, :],
+                        lhsT=xc_wd[:, P * t : P * (t + 1)].bitcast(FP8X4),
+                        lhsT_scale=xc_sd[:, P * t : P * (t + 1)],
+                        rhs=codes[:].bitcast(FP8X4),
+                        rhs_scale=scales[:],
+                        start=True,
+                        stop=True,
+                    )
+
+        def s_to_window(c, t):
+            start, w = CHUNKS[c]
+            per_bank = 1 if c == LAST else 512 // w
+            nc.scalar.activation(
+                s_win[t][:, start : start + w], s_ps[c, t // per_bank][:, t % per_bank, :], COPY, scale=0.0625
+            )
+
+        def s_to_own(c, b):
+            w = CHUNKS[c][1]
+            per_bank = 1 if c == LAST else 512 // w
+            nc.scalar.activation(
+                s_own[c][:, b * per_bank : (b + 1) * per_bank, :], s_ps[c, b][:], COPY, scale=0.0625
+            )
+
+        steps = [(c, t) for c in range(len(CHUNKS)) for t in range(PACK)]
+        for i, (c, t) in enumerate(steps):
+            tag = None
+            if (c, t) == (2, 0):
+                z_product(0)
+                tag = "z_bf0"
+            if (c, t) == (2, 3):
+                z_product(1)
+                for tt in range(PACK):
+                    s_to_window(1, tt)
+                s_to_own(0, 0)
+                tag = "z_bf1"
+            prod(c, t, tag)
+            if i > 0:
+                pc, pt = steps[i - 1]
+                zsum(pc, pt)
+                if pt == PACK - 1:
+                    z_round(pc)
+                    if pc == 1:
+                        for tt in range(PACK):
+                            s_to_window(0, tt)
+        zsum(LAST, PACK - 1)
+        z_round(LAST)
+        z_product(LAST)
+        s_to_window(LAST, 0)
+        s_to_window(LAST, 1)
+        s_to_own(0, 1)
+        s_to_window(LAST, 2)
+        s_to_window(LAST, 3)
+        s_to_own(1, 0)
+        for b in range(PACK):
+            s_to_own(LAST, b)
+
+        out_rows = out_0.rearrange("(p t) j -> p t j", t=PACK)
+        out_words = out_1[0].rearrange("p n t -> p (n t)").bitcast(I32)
+        o_f32 = [sb([P, PACK, w], F32, "o%d" % c) for c, (start, w) in enumerate(CHUNKS)]
+        o_scales = sb([P, S], U8, "o_scales")
+        d6 = {}
+        d5 = {}
+        top = {}
+        o_bf = {}
+
+        def diff(store, lst, name, c, t, tag=None):
+            start, w = CHUNKS[c]
+            tile = sb([P, w], F32, "%s_%d_%d" % (name, c, t), tag)
+            nc.vector.tensor_tensor(
+                tile[:], s_win[t][:].indirect(entries(lst, start, w)), s_own[c][:, t, :], ALU.subtract
+            )
+            store[c, t] = tile
+
+        def larger(c, t):
+            w = CHUNKS[c][1]
+            tile = sb([P, w], F32, "top%d_%d" % (c, t))
+            nc.vector.tensor_tensor(tile[:], d6[c, t][:], d5[c, t][:], ALU.max)
+            top[c, t] = tile
+
+        def result(c, t):
+            start, w = CHUNKS[c]
+            nc.vector.tensor_tensor(
+                o_f32[c][:, t, :], s_win[t][:].indirect(entries(n4_t, start, w)), top[c, t][:], ALU.subtract
+            )
+
+        def o_round(c):
+            start, w = CHUNKS[c]
+            o_bf[c] = sb([P, PACK * w], BF16, "o_bf%d" % c)
+            interleave(nc.vector.tensor_copy if c == LAST else nc.scalar.copy, o_bf[c], o_f32[c])
+            queue = nc.scalar if c == LAST else nc.sync
+            queue.dma_start(out_rows[:, :, start : start + w], o_f32[c][:])
+
+        def o_planes(c):
+            start, w = CHUNKS[c]
+            codes = sb([P, w], I32, "o_codes%d" % c)
+            nc.vector.quantize_mx(codes[:].bitcast(FP8X4), o_scales[:, start : start + w], o_bf[c][:])
+            nc.sync.dma_start(out_words[:, start : start + w], codes[:])
+
+        for i, (c, t) in enumerate(steps):
+            tag = None
+            if c > 0 and t == PACK - 1:
+                o_planes(c - 1)
+                tag = "o_bf%d" % (c - 1)
+            diff(d6, n6_t, "d6", c, t, tag)
+            if i > 0:
+                larger(*steps[i - 1])
+            diff(d5, n5_t, "d5", c, t)
+            if i > 0:
+                pc, pt = steps[i - 1]
+                result(pc, pt)
+                if pt == PACK - 1:
+                    o_round(pc)
+        larger(LAST, PACK - 1)
+        result(LAST, PACK - 1)
+        o_round(LAST)
+        o_planes(LAST)
+        for q in range(QUADS):
+            queue = nc.sync if q < 2 else nc.scalar
+            queue.dma_start(out_2[0, 4 * q : 4 * q + 4, :].bitcast(I32), o_scales[32 * q : 32 * q + 4, :].bitcast(I32))

@@ -1,6 +1,7 @@
 from contextlib import ExitStack
 
 import concourse.mybir as mybir
+from concourse.masks import make_identity
 
 K, T, S, H, J, C = 512, 2048, 512, 512, 512, 512
 FLOPS = 2 * K * H * S + 2 * K * C * S
@@ -14,14 +15,15 @@ U8 = mybir.dt.uint8
 FP8X4 = mybir.dt.float8_e4m3fn_x4
 FP4X4 = mybir.dt.float4_e2m1fn_x4
 ALU = mybir.AluOpType
+RELU = mybir.ActivationFunctionType.Relu
 COPY = mybir.ActivationFunctionType.Copy
 
 P = 128
 PACK = 4
 QUADS = 4
-CHUNKS = ((0, 256), (256, 128), (384, 128))
-LAST = len(CHUNKS) - 1
+WIN = 1024
 HALF = 256
+TURNED = 2
 
 
 def entries(offsets, start, width):
@@ -44,39 +46,36 @@ def tile_picked_candkindatrim_none_po_kernel(
             nc.sync.dma_start(offsets[:], src)
             return offsets
 
-        def load_scales(dst, src):
-            for q in range(QUADS):
+        def load_scales(dst, src, quads):
+            for q in quads:
                 nc.sync.dma_start(dst[32 * q : 32 * q + 4, :].bitcast(I32), src[0, 4 * q : 4 * q + 4, :].bitcast(I32))
-
-        def interleave(engine_copy, dst, src):
-            engine_copy(
-                dst[:].rearrange("p (c i t) -> p c t i", i=4, t=PACK),
-                src[:].rearrange("p t (c i) -> p c t i", i=4),
-            )
 
         xs = sb([P, T], U8, "xs")
         nc.vector.memset(xs[:].bitcast(I32), 0)
         w1s = sb([P, H], U8, "w1s")
-        nc.gpsimd.memset(w1s[:].bitcast(I32), 0)
+        nc.vector.memset(w1s[:].bitcast(I32), 0)
+        ident = sb([P, P], F32, "ident")
+        make_identity(nc, ident[:])
 
+        tab_rows = tab.rearrange("(p t) j -> p t j", t=PACK)
+        tabs = [sb([P, WIN], F32, "tab%d" % t) for t in range(PACK)]
         w1w = sb([P, 2 * H], U8, "w1w")
         nc.sync.dma_start(w1w[:].bitcast(I32), w1_words[0].bitcast(I32))
         n1_t = load_list(n1, "n1_t")
-        tab_rows = tab.rearrange("(p t) j -> p t j", t=PACK)
-        tabs = []
-        for t in range(PACK):
-            tile = sb([P, J], F32, "tab%d" % t)
-            nc.sync.dma_start(tile[:], tab_rows[:, t, :])
-            tabs.append(tile)
-        xw = sb([P, T], I32, "xw")
-        nc.sync.dma_start(xw[:], x_words[0].rearrange("p n t -> p (n t)").bitcast(I32))
+        nc.sync.dma_start(tabs[0][:, :J], tab_rows[:, 0, :])
+        for t in (1, 2):
+            nc.sync.dma_start(tabs[t][:, :J], tab_rows[:, t, :])
         offs_t = load_list(offs, "offs_t")
-        load_scales(xs, x_scales)
-        load_scales(w1s, w1_scales)
         gs_t = sb([P, PACK], F32, "gs_t")
         nc.sync.dma_start(gs_t[:], gs.rearrange("(p t) o -> p (t o)", t=PACK))
-        cand_t = load_list(cand, "cand_t")
         n3_t = load_list(n3, "n3_t")
+        load_scales(xs, x_scales, range(1))
+        xw = sb([P, T], I32, "xw")
+        nc.sync.dma_start(xw[:], x_words[0].rearrange("p n t -> p (n t)").bitcast(I32))
+        load_scales(xs, x_scales, range(1, QUADS))
+        load_scales(w1s, w1_scales, range(QUADS))
+        nc.sync.dma_start(tabs[3][:, :J], tab_rows[:, 3, :])
+        cand_t = load_list(cand, "cand_t")
         n2_t = load_list(n2, "n2_t")
         n6_t = load_list(n6, "n6_t")
         n5_t = load_list(n5, "n5_t")
@@ -88,18 +87,9 @@ def tile_picked_candkindatrim_none_po_kernel(
             w1w[:].rearrange("p (m t b) -> p t m b", t=PACK, b=2),
         )
 
-        kind1 = []
-        for t in range(PACK):
-            tile = sb([P, S], F32, "kind1_%d" % t)
-            for h in range(0, S, HALF):
-                nc.vector.tensor_copy(tile[:, h : h + HALF], tabs[t][:].indirect(entries(n1_t, h, HALF)))
-            kind1.append(tile)
-
-        tabg = []
-        for t in range(PACK):
-            tile = sb([P, J], F32, "tabg%d" % t)
-            nc.scalar.activation(tile[:], tabs[t][:], COPY, scale=gs_t[:, t : t + 1])
-            tabg.append(tile)
+        kind1 = [sb([P, S], F32, "kind1_%d" % t) for t in range(PACK)]
+        for t in range(PACK - 1):
+            nc.vector.tensor_copy(kind1[t][:], tabs[t][:].indirect(n1_t[:]))
 
         xq_w = sb([P, S], I32, "xq_w")
         nc.vector.tensor_copy(xq_w[:].bitcast(U32), xw[:].bitcast(U32).indirect(offs_t[:]))
@@ -109,8 +99,16 @@ def tile_picked_candkindatrim_none_po_kernel(
         nc.vector.tensor_copy(
             w1s_d[:].rearrange("p (t m) -> p t m", t=PACK), w1s[:].rearrange("p (m t) -> p t m", t=PACK)
         )
+        nc.vector.tensor_copy(kind1[3][:], tabs[3][:].indirect(n1_t[:]))
+        xc_w = sb([P, C], I32, "xc_w")
+        nc.vector.tensor_copy(xc_w[:].bitcast(U32), xw[:].bitcast(U32).indirect(cand_t[:]))
+        xc_wd = sb([P, C], I32, "xc_wd")
+        nc.vector.tensor_copy(
+            xc_wd[:].rearrange("p (t m) -> p t m", t=PACK), xc_w[:].rearrange("p (m t) -> p t m", t=PACK)
+        )
 
         ys = []
+        tabg = []
         for t in range(PACK):
             bank = psum.tile([P, S], F32, name="y_ps%d" % t, tag="bank%d" % t)
             nc.tensor.matmul_mx(
@@ -122,178 +120,167 @@ def tile_picked_candkindatrim_none_po_kernel(
                 start=True,
                 stop=True,
             )
-            tile = sb([P, S], F32, "y%d" % t)
-            nc.scalar.activation(tile[:], bank[:], COPY, scale=gs_t[:, t : t + 1])
+            tile = sb([P, WIN], F32, "y%d" % t)
+            nc.scalar.activation(tile[:, :S], bank[:], COPY, scale=gs_t[:, t : t + 1])
             ys.append(tile)
+            tile = sb([P, WIN], F32, "tabg%d" % t)
+            nc.scalar.activation(tile[:, :J], tabs[t][:, :J], COPY, scale=gs_t[:, t : t + 1])
+            tabg.append(tile)
 
-        xc_w = sb([P, C], I32, "xc_w")
-        nc.vector.tensor_copy(xc_w[:].bitcast(U32), xw[:].bitcast(U32).indirect(cand_t[:]))
-        xc_s = sb([P, C], U8, "xc_s")
+        z_f32 = [sb([P, 2, S], F32, "z_f32_%d" % pair) for pair in range(2)]
+        prods = [sb([P, S], F32, "prod%d" % t) for t in range(PACK)]
+
+        def zsum(t, start=0, w=S):
+            cols = slice(start, start + w)
+            nc.vector.tensor_tensor(
+                z_f32[t // 2][:, t % 2, cols], tabg[t][:].indirect(entries(n2_t, start, w)), prods[t][:, cols], ALU.add
+            )
+
+        halves = range(S // HALF)
+        z_bf = [sb([P, PACK * HALF], BF16, "z_bf%d" % h) for h in halves]
+
+        def round_pair(engine_copy, dst, src, pair, h):
+            engine_copy(
+                dst[h][:].rearrange("p (j t) -> p j t", t=PACK)[:, :, 2 * pair : 2 * pair + 2],
+                src[pair][:, :, h * HALF : (h + 1) * HALF].rearrange("p t j -> p j t"),
+            )
+
+        for t in range(PACK):
+            nc.vector.tensor_tensor(prods[t][:], ys[t][:].indirect(n3_t[:]), kind1[t][:], ALU.mult)
+            if t > 0:
+                zsum(t - 1)
+            if t == 2:
+                for h in halves:
+                    round_pair(nc.scalar.copy, z_bf, z_f32, 0, h)
+        for h in halves:
+            zsum(PACK - 1, h * HALF, HALF)
+            round_pair(nc.scalar.copy, z_bf, z_f32, 1, h)
+
+        xc_s = sb([P, C], U8, "xc_s", "tabg3")
         nc.vector.tensor_copy(xc_s[:], xs[:].indirect(cand_t[:]))
-        xc_wd = sb([P, C], I32, "xc_wd")
-        nc.vector.tensor_copy(
-            xc_wd[:].rearrange("p (t m) -> p t m", t=PACK), xc_w[:].rearrange("p (m t) -> p t m", t=PACK)
-        )
-        xc_sd = sb([P, C], U8, "xc_sd")
-        nc.vector.tensor_copy(
-            xc_sd[:].rearrange("p (t m) -> p t m", t=PACK), xc_s[:].rearrange("p (m t) -> p t m", t=PACK)
-        )
+        z_codes = [sb([P, HALF], U32, "z_codes%d" % h) for h in halves]
+        z_scales = [sb([P, HALF], U8, "z_scales%d" % h) for h in halves]
+        xc_planes = xc_s[:].rearrange("p (m t) -> p t m", t=PACK)
+        nc.vector.quantize_mx(z_codes[0][:].bitcast(FP8X4), z_scales[0][:], z_bf[0][:])
+        first_sd = sb([P, P], U8, "first_sd")
+        nc.vector.tensor_copy(first_sd[:], xc_planes[:, 0, :])
+        nc.vector.quantize_mx(z_codes[1][:].bitcast(FP8X4), z_scales[1][:], z_bf[1][:])
+        rest_sd = sb([P, (PACK - 1) * P], U8, "rest_sd", "z_bf1")
+        nc.vector.tensor_copy(rest_sd[:, :P], xc_planes[:, 1, :])
+        nc.vector.tensor_copy(rest_sd[:, P:].rearrange("p (t m) -> p t m", m=P), xc_planes[:, 2:, :])
+        xc_sd = [first_sd[:]] + [rest_sd[:, P * t : P * (t + 1)] for t in range(PACK - 1)]
 
-        z_f32 = [sb([P, PACK, w], F32, "z%d" % c) for c, (start, w) in enumerate(CHUNKS)]
-        s_win = [sb([P, S], F32, "s_win%d" % t) for t in range(PACK)]
-        s_own = [sb([P, PACK, w], F32, "s_own%d" % c) for c, (start, w) in enumerate(CHUNKS)]
-        prods = {}
-        z_bf = {}
+        s_win = [sb([P, WIN if t < PACK - 1 else S], F32, "s_win%d" % t) for t in range(PACK)]
+        s_own = {t: sb([P, S], F32, "s_own%d" % t) for t in range(TURNED, PACK)}
         s_ps = {}
-
-        def prod(c, t, tag=None):
-            start, w = CHUNKS[c]
-            tile = sb([P, w], F32, "prod%d_%d" % (c, t), tag)
-            nc.vector.tensor_tensor(
-                tile[:], ys[t][:].indirect(entries(n3_t, start, w)), kind1[t][:, start : start + w], ALU.mult
-            )
-            prods[c, t] = tile
-
-        def zsum(c, t):
-            start, w = CHUNKS[c]
-            nc.vector.tensor_tensor(
-                z_f32[c][:, t, :], tabg[t][:].indirect(entries(n2_t, start, w)), prods[c, t][:], ALU.add
-            )
-
-        def z_round(c):
-            w = CHUNKS[c][1]
-            z_bf[c] = sb([P, PACK * w], BF16, "z_bf%d" % c)
-            interleave(nc.vector.tensor_copy if c == LAST else nc.scalar.copy, z_bf[c], z_f32[c])
-
-        def z_product(c):
-            w = CHUNKS[c][1]
-            codes = sb([P, w], U32, "z_codes%d" % c)
-            scales = sb([P, w], U8, "z_scales%d" % c)
-            nc.vector.quantize_mx(codes[:].bitcast(FP8X4), scales[:], z_bf[c][:])
-            per_bank = 1 if c == LAST else 512 // w
-            first_bank = (4, 6, 0)[c]
-            for b in range(PACK // per_bank):
-                bank = psum.tile([P, per_bank, w], F32, name="s_ps%d_%d" % (c, b), tag="bank%d" % (first_bank + b))
-                s_ps[c, b] = bank
-                for i in range(per_bank):
-                    t = b * per_bank + i
-                    nc.tensor.matmul_mx(
-                        bank[:, i, :],
-                        lhsT=xc_wd[:, P * t : P * (t + 1)].bitcast(FP8X4),
-                        lhsT_scale=xc_sd[:, P * t : P * (t + 1)],
-                        rhs=codes[:].bitcast(FP8X4),
-                        rhs_scale=scales[:],
-                        start=True,
-                        stop=True,
-                    )
-
-        def s_to_window(c, t):
-            start, w = CHUNKS[c]
-            per_bank = 1 if c == LAST else 512 // w
-            nc.scalar.activation(
-                s_win[t][:, start : start + w], s_ps[c, t // per_bank][:, t % per_bank, :], COPY, scale=0.0625
-            )
-
-        def s_to_own(c, b):
-            w = CHUNKS[c][1]
-            per_bank = 1 if c == LAST else 512 // w
-            nc.scalar.activation(
-                s_own[c][:, b * per_bank : (b + 1) * per_bank, :], s_ps[c, b][:], COPY, scale=0.0625
-            )
-
-        steps = [(c, t) for c in range(len(CHUNKS)) for t in range(PACK)]
-        for i, (c, t) in enumerate(steps):
-            tag = None
-            if (c, t) == (2, 0):
-                z_product(0)
-                tag = "z_bf0"
-            if (c, t) == (2, 3):
-                z_product(1)
-                for tt in range(PACK):
-                    s_to_window(1, tt)
-                s_to_own(0, 0)
-                tag = "z_bf1"
-            prod(c, t, tag)
-            if i > 0:
-                pc, pt = steps[i - 1]
-                zsum(pc, pt)
-                if pt == PACK - 1:
-                    z_round(pc)
-                    if pc == 1:
-                        for tt in range(PACK):
-                            s_to_window(0, tt)
-        zsum(LAST, PACK - 1)
-        z_round(LAST)
-        z_product(LAST)
-        s_to_window(LAST, 0)
-        s_to_window(LAST, 1)
-        s_to_own(0, 1)
-        s_to_window(LAST, 2)
-        s_to_window(LAST, 3)
-        s_to_own(1, 0)
-        for b in range(PACK):
-            s_to_own(LAST, b)
+        for t in range(PACK):
+            for h in halves:
+                s_ps[t, h] = psum.tile([P, HALF], F32, name="s_ps%d_%d" % (t, h), tag="bank%d" % ((4 + 2 * t + h) % 8))
+                nc.tensor.matmul_mx(
+                    s_ps[t, h][:],
+                    lhsT=xc_wd[:, P * t : P * (t + 1)].bitcast(FP8X4),
+                    lhsT_scale=xc_sd[t],
+                    rhs=z_codes[h][:].bitcast(FP8X4),
+                    rhs_scale=z_scales[h][:],
+                    start=True,
+                    stop=True,
+                )
+        for t in range(PACK):
+            for h in halves:
+                cols = slice(h * HALF, (h + 1) * HALF)
+                nc.scalar.activation(s_win[t][:, cols], s_ps[t, h][:], COPY, scale=-0.0625 if t < TURNED else 0.0625)
+                if t >= TURNED:
+                    nc.scalar.activation(s_own[t][:, cols], s_ps[t, h][:], COPY, scale=0.0625)
 
         out_rows = out_0.rearrange("(p t) j -> p t j", t=PACK)
         out_words = out_1[0].rearrange("p n t -> p (n t)").bitcast(I32)
-        o_f32 = [sb([P, PACK, w], F32, "o%d" % c) for c, (start, w) in enumerate(CHUNKS)]
+        o_f32 = [sb([P, 2, S], F32, "o_f32_%d" % pair) for pair in range(2)]
         o_scales = sb([P, S], U8, "o_scales")
+        o_bf = [sb([P, PACK * HALF], BF16, "o_bf%d" % h) for h in halves]
+
+        at5 = [sb([P, S], F32, "at5_%d" % t) for t in range(TURNED)]
+        gap = [sb([P, S], F32, "gap%d" % t) for t in range(TURNED)]
+        rest = [sb([P, S], F32, "rest%d" % t) for t in range(TURNED)]
+
+        def turned_sum(t):
+            excess = sb([P, S], F32, "excess%d" % t)
+            nc.scalar.activation(excess[:], gap[t][:], RELU, scale=-1.0)
+            total = psum.tile([P, S], F32, name="total%d" % t, tag="bank%d" % ((4 + 2 * t) % 8))
+            for lo in range(0, S, P):
+                terms = (s_win[t], excess, rest[t])
+                for k, term in enumerate(terms):
+                    nc.tensor.matmul(
+                        total[:, lo : lo + P],
+                        term[:, lo : lo + P],
+                        ident[:],
+                        start=(k == 0),
+                        stop=(k == len(terms) - 1),
+                        is_transpose=True,
+                    )
+            held = sb([P, S], F32, "held%d" % t)
+            nc.scalar.activation(held[:], total[:], COPY, scale=-1.0)
+            back = psum.tile([P, S], F32, name="back%d" % t, tag="bank%d" % ((5 + 2 * t) % 8))
+            for lo in range(0, S, P):
+                nc.tensor.transpose(back[:, lo : lo + P], held[:, lo : lo + P], ident[:])
+            nc.scalar.copy(o_f32[t // 2][:, t % 2, :], back[:])
+            nc.sync.dma_start(out_rows[:, t, :], o_f32[t // 2][:, t % 2, :])
+
+        nc.vector.tensor_copy(at5[0][:], s_win[0][:].indirect(n5_t[:]))
+        for t in range(TURNED):
+            if t + 1 < TURNED:
+                nc.vector.tensor_copy(at5[t + 1][:], s_win[t + 1][:].indirect(n5_t[:]))
+            nc.vector.tensor_tensor(gap[t][:], s_win[t][:].indirect(n6_t[:]), at5[t][:], ALU.subtract)
+            nc.vector.tensor_tensor(rest[t][:], s_win[t][:].indirect(n4_t[:]), at5[t][:], ALU.subtract)
+            turned_sum(t)
+            if t == 1:
+                for h in halves:
+                    round_pair(nc.scalar.copy, o_bf, o_f32, 0, h)
+
+        steps = [(t, 0, S) for t in range(TURNED, PACK - 1)] + [(PACK - 1, h * HALF, HALF) for h in halves]
         d6 = {}
         d5 = {}
         top = {}
-        o_bf = {}
 
-        def diff(store, lst, name, c, t, tag=None):
-            start, w = CHUNKS[c]
-            tile = sb([P, w], F32, "%s_%d_%d" % (name, c, t), tag)
+        def diff(store, lst, name, step):
+            t, start, w = step
+            tag = "d5_%d_0" % t if name == "d5" and step == steps[-1] else None
+            store[step] = sb([P, w], F32, "%s_%d_%d" % (name, t, start), tag)
             nc.vector.tensor_tensor(
-                tile[:], s_win[t][:].indirect(entries(lst, start, w)), s_own[c][:, t, :], ALU.subtract
-            )
-            store[c, t] = tile
-
-        def larger(c, t):
-            w = CHUNKS[c][1]
-            tile = sb([P, w], F32, "top%d_%d" % (c, t))
-            nc.vector.tensor_tensor(tile[:], d6[c, t][:], d5[c, t][:], ALU.max)
-            top[c, t] = tile
-
-        def result(c, t):
-            start, w = CHUNKS[c]
-            nc.vector.tensor_tensor(
-                o_f32[c][:, t, :], s_win[t][:].indirect(entries(n4_t, start, w)), top[c, t][:], ALU.subtract
+                store[step][:], s_win[t][:].indirect(entries(lst, start, w)), s_own[t][:, start : start + w], ALU.subtract
             )
 
-        def o_round(c):
-            start, w = CHUNKS[c]
-            o_bf[c] = sb([P, PACK * w], BF16, "o_bf%d" % c)
-            interleave(nc.vector.tensor_copy if c == LAST else nc.scalar.copy, o_bf[c], o_f32[c])
-            queue = nc.scalar if c == LAST else nc.sync
-            queue.dma_start(out_rows[:, :, start : start + w], o_f32[c][:])
+        def larger(step):
+            t, start, w = step
+            tag = "held%d" % (TURNED - 1) if step == steps[-2] else None
+            top[step] = sb([P, w], F32, "top%d_%d" % (t, start), tag)
+            nc.vector.tensor_tensor(top[step][:], d6[step][:], d5[step][:], ALU.max)
 
-        def o_planes(c):
-            start, w = CHUNKS[c]
-            codes = sb([P, w], I32, "o_codes%d" % c)
-            nc.vector.quantize_mx(codes[:].bitcast(FP8X4), o_scales[:, start : start + w], o_bf[c][:])
-            nc.sync.dma_start(out_words[:, start : start + w], codes[:])
+        def result(step):
+            t, start, w = step
+            cols = slice(start, start + w)
+            dst = o_f32[t // 2][:, t % 2, cols]
+            nc.vector.tensor_tensor(dst, s_win[t][:].indirect(entries(n4_t, start, w)), top[step][:], ALU.subtract)
+            nc.sync.dma_start(out_rows[:, t, cols], dst)
 
-        for i, (c, t) in enumerate(steps):
-            tag = None
-            if c > 0 and t == PACK - 1:
-                o_planes(c - 1)
-                tag = "o_bf%d" % (c - 1)
-            diff(d6, n6_t, "d6", c, t, tag)
+        def o_planes(h):
+            codes = sb([P, HALF], I32, "o_codes%d" % h)
+            cols = slice(h * HALF, (h + 1) * HALF)
+            nc.vector.quantize_mx(codes[:].bitcast(FP8X4), o_scales[:, cols], o_bf[h][:])
+            nc.sync.dma_start(out_words[:, cols], codes[:])
+
+        for i, step in enumerate(steps):
+            diff(d6, n6_t, "d6", step)
             if i > 0:
-                larger(*steps[i - 1])
-            diff(d5, n5_t, "d5", c, t)
+                larger(steps[i - 1])
+            diff(d5, n5_t, "d5", step)
             if i > 0:
-                pc, pt = steps[i - 1]
-                result(pc, pt)
-                if pt == PACK - 1:
-                    o_round(pc)
-        larger(LAST, PACK - 1)
-        result(LAST, PACK - 1)
-        o_round(LAST)
-        o_planes(LAST)
+                result(steps[i - 1])
+        round_pair(nc.scalar.copy, o_bf, o_f32, 1, 0)
+        larger(steps[-1])
+        result(steps[-1])
+        round_pair(nc.vector.tensor_copy, o_bf, o_f32, 1, 1)
+        o_planes(0)
+        o_planes(1)
         for q in range(QUADS):
             queue = nc.sync if q < 2 else nc.scalar
             queue.dma_start(out_2[0, 4 * q : 4 * q + 4, :].bitcast(I32), o_scales[32 * q : 32 * q + 4, :].bitcast(I32))

from contextlib import ExitStack

import concourse.mybir as mybir
from concourse.masks import make_identity

K, T, S, H, J, C = 512, 2048, 512, 512, 512, 512
FLOPS = 2 * K * H * S + 2 * K * C * S

F32 = mybir.dt.float32
BF16 = mybir.dt.bfloat16
I32 = mybir.dt.int32
U32 = mybir.dt.uint32
U16 = mybir.dt.uint16
U8 = mybir.dt.uint8
FP8X4 = mybir.dt.float8_e4m3fn_x4
FP4X4 = mybir.dt.float4_e2m1fn_x4
ALU = mybir.AluOpType
RELU = mybir.ActivationFunctionType.Relu
COPY = mybir.ActivationFunctionType.Copy

P = 128
PACK = 4
QUADS = 4
WIN = 1024
HALF = 256
TURNED = 2


def entries(offsets, start, width):
    return offsets[:, start // 16 : (start + width) // 16]


def tile_picked_candkindatrim_none_po_kernel(
    tc, x_words, x_scales, w1_words, w1_scales, tab, gs, offs, n1, n2, n3, cand, n4, n5, n6, out_0, out_1, out_2
):
    nc = tc.nc
    with ExitStack() as ctx:
        keep = ctx.enter_context(tc.tile_pool(name="keep", bufs=1))
        psum = ctx.enter_context(tc.psum_pool(name="psum", bufs=1))

        def sb(shape, dtype, name, tag=None):
            return keep.tile(shape, dtype, name=name, tag=tag or name, align_bytes=64)

        def load_list(src, name):
            offsets = keep.tile([P, S // 16], U16, name=name)
            nc.sync.dma_start(offsets[:], src)
            return offsets

        def load_scales(dst, src, quads):
            for q in quads:
                nc.sync.dma_start(dst[32 * q : 32 * q + 4, :].bitcast(I32), src[0, 4 * q : 4 * q + 4, :].bitcast(I32))

        xs = sb([P, T], U8, "xs")
        nc.vector.memset(xs[:].bitcast(I32), 0)
        w1s = sb([P, H], U8, "w1s")
        nc.vector.memset(w1s[:].bitcast(I32), 0)
        ident = sb([P, P], F32, "ident")
        make_identity(nc, ident[:])

        tab_rows = tab.rearrange("(p t) j -> p t j", t=PACK)
        tabs = [sb([P, WIN], F32, "tab%d" % t) for t in range(PACK)]
        w1w = sb([P, 2 * H], U8, "w1w")
        nc.sync.dma_start(w1w[:].bitcast(I32), w1_words[0].bitcast(I32))
        n1_t = load_list(n1, "n1_t")
        nc.sync.dma_start(tabs[0][:, :J], tab_rows[:, 0, :])
        for t in (1, 2):
            nc.sync.dma_start(tabs[t][:, :J], tab_rows[:, t, :])
        offs_t = load_list(offs, "offs_t")
        gs_t = sb([P, PACK], F32, "gs_t")
        nc.sync.dma_start(gs_t[:], gs.rearrange("(p t) o -> p (t o)", t=PACK))
        n3_t = load_list(n3, "n3_t")
        load_scales(xs, x_scales, range(1))
        xw = sb([P, T], I32, "xw")
        nc.sync.dma_start(xw[:], x_words[0].rearrange("p n t -> p (n t)").bitcast(I32))
        load_scales(xs, x_scales, range(1, QUADS))
        load_scales(w1s, w1_scales, range(QUADS))
        nc.sync.dma_start(tabs[3][:, :J], tab_rows[:, 3, :])
        cand_t = load_list(cand, "cand_t")
        n2_t = load_list(n2, "n2_t")
        n6_t = load_list(n6, "n6_t")
        n5_t = load_list(n5, "n5_t")
        n4_t = load_list(n4, "n4_t")

        w1w_d = sb([P, 2 * H], U8, "w1w_d")
        nc.vector.tensor_copy(
            w1w_d[:].rearrange("p (t m b) -> p t m b", t=PACK, b=2),
            w1w[:].rearrange("p (m t b) -> p t m b", t=PACK, b=2),
        )

        kind1 = [sb([P, S], F32, "kind1_%d" % t) for t in range(PACK)]
        for t in range(PACK - 1):
            nc.vector.tensor_copy(kind1[t][:], tabs[t][:].indirect(n1_t[:]))

        xq_w = sb([P, S], I32, "xq_w")
        nc.vector.tensor_copy(xq_w[:].bitcast(U32), xw[:].bitcast(U32).indirect(offs_t[:]))
        xq_s = sb([P, S], U8, "xq_s")
        nc.vector.tensor_copy(xq_s[:], xs[:].indirect(offs_t[:]))
        w1s_d = sb([P, H], U8, "w1s_d")
        nc.vector.tensor_copy(
            w1s_d[:].rearrange("p (t m) -> p t m", t=PACK), w1s[:].rearrange("p (m t) -> p t m", t=PACK)
        )
        nc.vector.tensor_copy(kind1[3][:], tabs[3][:].indirect(n1_t[:]))
        xc_w = sb([P, C], I32, "xc_w")
        nc.vector.tensor_copy(xc_w[:].bitcast(U32), xw[:].bitcast(U32).indirect(cand_t[:]))
        xc_wd = sb([P, C], I32, "xc_wd")
        nc.vector.tensor_copy(
            xc_wd[:].rearrange("p (t m) -> p t m", t=PACK), xc_w[:].rearrange("p (m t) -> p t m", t=PACK)
        )

        ys = []
        tabg = []
        for t in range(PACK):
            bank = psum.tile([P, S], F32, name="y_ps%d" % t, tag="bank%d" % t)
            nc.tensor.matmul_mx(
                bank[:],
                lhsT=w1w_d[:, 2 * P * t : 2 * P * (t + 1)].bitcast(FP4X4),
                lhsT_scale=w1s_d[:, P * t : P * (t + 1)],
                rhs=xq_w[:].bitcast(FP8X4),
                rhs_scale=xq_s[:],
                start=True,
                stop=True,
            )
            tile = sb([P, WIN], F32, "y%d" % t)
            nc.scalar.activation(tile[:, :S], bank[:], COPY, scale=gs_t[:, t : t + 1])
            ys.append(tile)
            tile = sb([P, WIN], F32, "tabg%d" % t)
            nc.scalar.activation(tile[:, :J], tabs[t][:, :J], COPY, scale=gs_t[:, t : t + 1])
            tabg.append(tile)

        z_f32 = [sb([P, 2, S], F32, "z_f32_%d" % pair) for pair in range(2)]
        prods = [sb([P, S], F32, "prod%d" % t) for t in range(PACK)]

        def zsum(t, start=0, w=S):
            cols = slice(start, start + w)
            nc.vector.tensor_tensor(
                z_f32[t // 2][:, t % 2, cols], tabg[t][:].indirect(entries(n2_t, start, w)), prods[t][:, cols], ALU.add
            )

        halves = range(S // HALF)
        z_bf = [sb([P, PACK * HALF], BF16, "z_bf%d" % h) for h in halves]

        def round_pair(engine_copy, dst, src, pair, h):
            engine_copy(
                dst[h][:].rearrange("p (j t) -> p j t", t=PACK)[:, :, 2 * pair : 2 * pair + 2],
                src[pair][:, :, h * HALF : (h + 1) * HALF].rearrange("p t j -> p j t"),
            )

        for t in range(PACK):
            nc.vector.tensor_tensor(prods[t][:], ys[t][:].indirect(n3_t[:]), kind1[t][:], ALU.mult)
            if t > 0:
                zsum(t - 1)
            if t == 2:
                for h in halves:
                    round_pair(nc.scalar.copy, z_bf, z_f32, 0, h)
        for h in halves:
            zsum(PACK - 1, h * HALF, HALF)
            round_pair(nc.scalar.copy, z_bf, z_f32, 1, h)

        xc_s = sb([P, C], U8, "xc_s", "tabg3")
        nc.vector.tensor_copy(xc_s[:], xs[:].indirect(cand_t[:]))
        z_codes = [sb([P, HALF], U32, "z_codes%d" % h) for h in halves]
        z_scales = [sb([P, HALF], U8, "z_scales%d" % h) for h in halves]
        xc_planes = xc_s[:].rearrange("p (m t) -> p t m", t=PACK)
        nc.vector.quantize_mx(z_codes[0][:].bitcast(FP8X4), z_scales[0][:], z_bf[0][:])
        first_sd = sb([P, P], U8, "first_sd")
        nc.vector.tensor_copy(first_sd[:], xc_planes[:, 0, :])
        nc.vector.quantize_mx(z_codes[1][:].bitcast(FP8X4), z_scales[1][:], z_bf[1][:])
        rest_sd = sb([P, (PACK - 1) * P], U8, "rest_sd", "z_bf1")
        nc.vector.tensor_copy(rest_sd[:, :P], xc_planes[:, 1, :])
        nc.vector.tensor_copy(rest_sd[:, P:].rearrange("p (t m) -> p t m", m=P), xc_planes[:, 2:, :])
        xc_sd = [first_sd[:]] + [rest_sd[:, P * t : P * (t + 1)] for t in range(PACK - 1)]

        s_win = [sb([P, WIN if t < PACK - 1 else S], F32, "s_win%d" % t) for t in range(PACK)]
        s_own = {t: sb([P, S], F32, "s_own%d" % t) for t in range(TURNED, PACK)}
        s_ps = {}
        for t in range(PACK):
            for h in halves:
                s_ps[t, h] = psum.tile([P, HALF], F32, name="s_ps%d_%d" % (t, h), tag="bank%d" % ((4 + 2 * t + h) % 8))
                nc.tensor.matmul_mx(
                    s_ps[t, h][:],
                    lhsT=xc_wd[:, P * t : P * (t + 1)].bitcast(FP8X4),
                    lhsT_scale=xc_sd[t],
                    rhs=z_codes[h][:].bitcast(FP8X4),
                    rhs_scale=z_scales[h][:],
                    start=True,
                    stop=True,
                )
        for t in range(PACK):
            for h in halves:
                cols = slice(h * HALF, (h + 1) * HALF)
                nc.scalar.activation(s_win[t][:, cols], s_ps[t, h][:], COPY, scale=-0.0625 if t < TURNED else 0.0625)
                if t >= TURNED:
                    nc.scalar.activation(s_own[t][:, cols], s_ps[t, h][:], COPY, scale=0.0625)

        out_rows = out_0.rearrange("(p t) j -> p t j", t=PACK)
        out_words = out_1[0].rearrange("p n t -> p (n t)").bitcast(I32)
        o_f32 = [sb([P, 2, S], F32, "o_f32_%d" % pair) for pair in range(2)]
        o_scales = sb([P, S], U8, "o_scales")
        o_bf = [sb([P, PACK * HALF], BF16, "o_bf%d" % h) for h in halves]

        at5 = [sb([P, S], F32, "at5_%d" % t) for t in range(TURNED)]
        gap = [sb([P, S], F32, "gap%d" % t) for t in range(TURNED)]
        rest = [sb([P, S], F32, "rest%d" % t) for t in range(TURNED)]

        def turned_sum(t):
            excess = sb([P, S], F32, "excess%d" % t)
            nc.scalar.activation(excess[:], gap[t][:], RELU, scale=-1.0)
            total = psum.tile([P, S], F32, name="total%d" % t, tag="bank%d" % ((4 + 2 * t) % 8))
            for lo in range(0, S, P):
                terms = (s_win[t], excess, rest[t])
                for k, term in enumerate(terms):
                    nc.tensor.matmul(
                        total[:, lo : lo + P],
                        term[:, lo : lo + P],
                        ident[:],
                        start=(k == 0),
                        stop=(k == len(terms) - 1),
                        is_transpose=True,
                    )
            held = sb([P, S], F32, "held%d" % t)
            nc.scalar.activation(held[:], total[:], COPY, scale=-1.0)
            back = psum.tile([P, S], F32, name="back%d" % t, tag="bank%d" % ((5 + 2 * t) % 8))
            for lo in range(0, S, P):
                nc.tensor.transpose(back[:, lo : lo + P], held[:, lo : lo + P], ident[:])
            nc.scalar.copy(o_f32[t // 2][:, t % 2, :], back[:])
            nc.sync.dma_start(out_rows[:, t, :], o_f32[t // 2][:, t % 2, :])

        nc.vector.tensor_copy(at5[0][:], s_win[0][:].indirect(n5_t[:]))
        for t in range(TURNED):
            if t + 1 < TURNED:
                nc.vector.tensor_copy(at5[t + 1][:], s_win[t + 1][:].indirect(n5_t[:]))
            nc.vector.tensor_tensor(gap[t][:], s_win[t][:].indirect(n6_t[:]), at5[t][:], ALU.subtract)
            nc.vector.tensor_tensor(rest[t][:], s_win[t][:].indirect(n4_t[:]), at5[t][:], ALU.subtract)
            turned_sum(t)
            if t == 1:
                for h in halves:
                    round_pair(nc.scalar.copy, o_bf, o_f32, 0, h)

        steps = [(t, 0, S) for t in range(TURNED, PACK - 1)] + [(PACK - 1, h * HALF, HALF) for h in halves]
        d6 = {}
        d5 = {}
        top = {}

        def diff(store, lst, name, step):
            t, start, w = step
            tag = "d5_%d_0" % t if name == "d5" and step == steps[-1] else None
            store[step] = sb([P, w], F32, "%s_%d_%d" % (name, t, start), tag)
            nc.vector.tensor_tensor(
                store[step][:], s_win[t][:].indirect(entries(lst, start, w)), s_own[t][:, start : start + w], ALU.subtract
            )

        def larger(step):
            t, start, w = step
            tag = "held%d" % (TURNED - 1) if step == steps[-2] else None
            top[step] = sb([P, w], F32, "top%d_%d" % (t, start), tag)
            nc.vector.tensor_tensor(top[step][:], d6[step][:], d5[step][:], ALU.max)

        def result(step):
            t, start, w = step
            cols = slice(start, start + w)
            dst = o_f32[t // 2][:, t % 2, cols]
            nc.vector.tensor_tensor(dst, s_win[t][:].indirect(entries(n4_t, start, w)), top[step][:], ALU.subtract)
            nc.sync.dma_start(out_rows[:, t, cols], dst)

        def o_planes(h):
            codes = sb([P, HALF], I32, "o_codes%d" % h)
            cols = slice(h * HALF, (h + 1) * HALF)
            nc.vector.quantize_mx(codes[:].bitcast(FP8X4), o_scales[:, cols], o_bf[h][:])
            nc.sync.dma_start(out_words[:, cols], codes[:])

        for i, step in enumerate(steps):
            diff(d6, n6_t, "d6", step)
            if i > 0:
                larger(steps[i - 1])
            diff(d5, n5_t, "d5", step)
            if i > 0:
                result(steps[i - 1])
        round_pair(nc.scalar.copy, o_bf, o_f32, 1, 0)
        larger(steps[-1])
        result(steps[-1])
        round_pair(nc.vector.tensor_copy, o_bf, o_f32, 1, 1)
        o_planes(0)
        o_planes(1)
        for q in range(QUADS):
            queue = nc.sync if q < 2 else nc.scalar
            queue.dma_start(out_2[0, 4 * q : 4 * q + 4, :].bitcast(I32), o_scales[32 * q : 32 * q + 4, :].bitcast(I32))
